import numpy as np
import ml_dtypes

BF16 = ml_dtypes.bfloat16


def bf(x):
    return np.asarray(x, np.float32).astype(BF16)


def f32(x):
    return np.asarray(x, np.float32)


def f64(x):
    return np.asarray(x).astype(np.float64)


def striped(idx):
    return np.tile(idx.reshape(-1, 16).T, (8, 1))


def rows(idx, k):
    return np.tile(idx, (k, 1))


def look(tab, idx):
    return np.take_along_axis(f64(tab), rows(idx, len(tab)), axis=1)


K, S, D, V, N, M = 512, 2048, 1, 512, 512, 512


def setup_inputs():
    return {"tab": bf(0.7 * np.random.standard_normal((D, K, S))), "base": bf(np.random.standard_normal((K, V))), "w": bf(np.random.standard_normal((K, M)) / np.sqrt(K)), "offs": striped(np.random.randint(0, S, N))}


def reference(tab, base, w, offs):
    idx = offs[:16].T.reshape(-1)
    x = f64(base) + sum(look(tab[d], idx[d * V:(d + 1) * V]) for d in range(D))
    y = f64(w).T @ x
    return y

@@ -1,0 +1,51 @@
+import concourse.mybir as mybir
+
+BF16, F32, U16 = mybir.dt.bfloat16, mybir.dt.float32, mybir.dt.uint16
+
+P = 128
+R = 512
+S = 2048
+N = 512
+M = 512
+FLOPS = 2 * R * M * N + R * N
+
+
+def tile_lookup_res_add_none_kernel(tc, tab, base, w, offs, out):
+    nc = tc.nc
+    row_blocks, out_blocks = R // P, M // P
+    tab_blocks = tab.rearrange("d (k p) s -> (d k) p s", p=P)
+    base_blocks = base.rearrange("(k p) n -> k p n", p=P)
+    w_blocks = w.rearrange("(k p) m -> k p m", p=P)
+    out_rows = out.rearrange("(m p) n -> m p n", p=P)
+
+    with (
+        tc.tile_pool(name="held", bufs=1) as held,
+        tc.tile_pool(name="blocks", bufs=row_blocks) as blocks,
+        tc.tile_pool(name="results", bufs=out_blocks) as results,
+        tc.psum_pool(name="psum", bufs=1) as psum,
+    ):
+        offsets = held.tile([P, N // 16], U16, name="offsets")
+        nc.sync.dma_start(offsets[:], offs)
+        banks = [psum.tile([P, N], F32, name=f"bank{m}") for m in range(out_blocks)]
+
+        for k in range(row_blocks):
+            window = blocks.tile([P, S], BF16, name="window")
+            base_block = blocks.tile([P, N], BF16, name="base_block")
+            weights = blocks.tile([P, M], BF16, name="weights")
+            nc.sync.dma_start(window[:], tab_blocks[k, :, :])
+            nc.sync.dma_start(base_block[:], base_blocks[k, :, :])
+            nc.sync.dma_start(weights[:], w_blocks[k, :, :])
+
+            x = blocks.tile([P, N], BF16, name="x")
+            nc.vector.tensor_tensor(x[:], window[:].indirect(offsets[:]), base_block[:], mybir.AluOpType.add)
+            for m in range(out_blocks):
+                nc.tensor.matmul(banks[m][:], weights[:, m * P : (m + 1) * P], x[:],
+                                 start=(k == 0), stop=(k == row_blocks - 1))
+
+        for m in range(out_blocks):
+            result = results.tile([P, N], F32, name="result")
+            if m % 2 == 0:
+                nc.scalar.copy(result[:], banks[m][:])
+            else:
+                nc.vector.tensor_copy(result[:], banks[m][:])
+            nc.sync.dma_start(out_rows[m, :, :], result[:])

@@ -13,33 +13,36 @@ FLOPS = 2 * R * M * N + R * N
 def tile_lookup_res_add_none_kernel(tc, tab, base, w, offs, out):
     nc = tc.nc
     row_blocks, out_blocks = R // P, M // P
-    tab_blocks = tab.rearrange("d (k p) s -> (d k) p s", p=P)
-    base_blocks = base.rearrange("(k p) n -> k p n", p=P)
-    w_blocks = w.rearrange("(k p) m -> k p m", p=P)
+    tab_blocks = tab.rearrange("d (p k) s -> (d k) p s", p=P)
+    base_rows = base.rearrange("(p k) n -> p (k n)", p=P)
+    w_rows = w.rearrange("(p k) m -> p (k m)", p=P)
     out_rows = out.rearrange("(m p) n -> m p n", p=P)
 
     with (
         tc.tile_pool(name="held", bufs=1) as held,
-        tc.tile_pool(name="blocks", bufs=row_blocks) as blocks,
+        tc.tile_pool(name="x_blocks", bufs=row_blocks) as x_blocks,
         tc.tile_pool(name="results", bufs=out_blocks) as results,
         tc.psum_pool(name="psum", bufs=1) as psum,
     ):
         offsets = held.tile([P, N // 16], U16, name="offsets")
         nc.sync.dma_start(offsets[:], offs)
+        windows = [held.tile([P, S], BF16, name=f"window{k}") for k in range(row_blocks)]
+        bases = held.tile([P, row_blocks * N], BF16, name="bases")
+        weights = held.tile([P, row_blocks * M], BF16, name="weights")
+        nc.sync.dma_start(windows[0][:], tab_blocks[0, :, :])
+        nc.sync.dma_start(bases[:], base_rows)
+        nc.sync.dma_start(weights[:], w_rows)
+        for k in range(1, row_blocks):
+            nc.sync.dma_start(windows[k][:], tab_blocks[k, :, :])
+
         banks = [psum.tile([P, N], F32, name=f"bank{m}") for m in range(out_blocks)]
 
         for k in range(row_blocks):
-            window = blocks.tile([P, S], BF16, name="window")
-            base_block = blocks.tile([P, N], BF16, name="base_block")
-            weights = blocks.tile([P, M], BF16, name="weights")
-            nc.sync.dma_start(window[:], tab_blocks[k, :, :])
-            nc.sync.dma_start(base_block[:], base_blocks[k, :, :])
-            nc.sync.dma_start(weights[:], w_blocks[k, :, :])
-
-            x = blocks.tile([P, N], BF16, name="x")
-            nc.vector.tensor_tensor(x[:], window[:].indirect(offsets[:]), base_block[:], mybir.AluOpType.add)
+            x = x_blocks.tile([P, N], BF16, name="x")
+            nc.vector.tensor_tensor(x[:], windows[k][:].indirect(offsets[:]), bases[:, k * N : (k + 1) * N],
+                                    mybir.AluOpType.add)
             for m in range(out_blocks):
-                nc.tensor.matmul(banks[m][:], weights[:, m * P : (m + 1) * P], x[:],
+                nc.tensor.matmul(banks[m][:], weights[:, k * M + m * P : k * M + (m + 1) * P], x[:],
                                  start=(k == 0), stop=(k == row_blocks - 1))
 
         for m in range(out_blocks):

@@ -7,6 +7,7 @@ R = 512
 S = 2048
 N = 512
 M = 512
+HALF = N // 2
 FLOPS = 2 * R * M * N + R * N
 
 
@@ -20,8 +21,8 @@ def tile_lookup_res_add_none_kernel(tc, tab, base, w, offs, out):
 
     with (
         tc.tile_pool(name="held", bufs=1) as held,
-        tc.tile_pool(name="x_blocks", bufs=row_blocks) as x_blocks,
-        tc.tile_pool(name="results", bufs=out_blocks) as results,
+        tc.tile_pool(name="x_halves", bufs=2 * row_blocks) as x_halves,
+        tc.tile_pool(name="results", bufs=2 * out_blocks) as results,
         tc.psum_pool(name="psum", bufs=1) as psum,
     ):
         offsets = held.tile([P, N // 16], U16, name="offsets")
@@ -35,20 +36,23 @@ def tile_lookup_res_add_none_kernel(tc, tab, base, w, offs, out):
         for k in range(1, row_blocks):
             nc.sync.dma_start(windows[k][:], tab_blocks[k, :, :])
 
-        banks = [psum.tile([P, N], F32, name=f"bank{m}") for m in range(out_blocks)]
+        banks = [[psum.tile([P, HALF], F32, name=f"bank{h}_{m}") for m in range(out_blocks)] for h in range(2)]
 
         for k in range(row_blocks):
-            x = x_blocks.tile([P, N], BF16, name="x")
-            nc.vector.tensor_tensor(x[:], windows[k][:].indirect(offsets[:]), bases[:, k * N : (k + 1) * N],
-                                    mybir.AluOpType.add)
-            for m in range(out_blocks):
-                nc.tensor.matmul(banks[m][:], weights[:, k * M + m * P : k * M + (m + 1) * P], x[:],
-                                 start=(k == 0), stop=(k == row_blocks - 1))
+            for h in range(2):
+                half_list = offsets[:, h * HALF // 16 : (h + 1) * HALF // 16]
+                x = x_halves.tile([P, HALF], BF16, name="x")
+                nc.vector.tensor_tensor(x[:], windows[k][:].indirect(half_list),
+                                        bases[:, k * N + h * HALF : k * N + (h + 1) * HALF], mybir.AluOpType.add)
+                for m in range(out_blocks):
+                    nc.tensor.matmul(banks[h][m][:], weights[:, k * M + m * P : k * M + (m + 1) * P], x[:],
+                                     start=(k == 0), stop=(k == row_blocks - 1))
 
-        for m in range(out_blocks):
-            result = results.tile([P, N], F32, name="result")
-            if m % 2 == 0:
-                nc.scalar.copy(result[:], banks[m][:])
-            else:
-                nc.vector.tensor_copy(result[:], banks[m][:])
-            nc.sync.dma_start(out_rows[m, :, :], result[:])
+        for h in range(2):
+            for m in range(out_blocks):
+                result = results.tile([P, HALF], F32, name="result")
+                if h == 0:
+                    nc.scalar.copy(result[:], banks[h][m][:])
+                else:
+                    nc.vector.tensor_copy(result[:], banks[h][m][:])
+                nc.sync.dma_start(out_rows[m, :, h * HALF : (h + 1) * HALF], result[:])

import concourse.mybir as mybir

BF16, F32, U16 = mybir.dt.bfloat16, mybir.dt.float32, mybir.dt.uint16

P = 128
R = 512
S = 2048
N = 512
M = 512
HALF = N // 2
FLOPS = 2 * R * M * N + R * N


def tile_lookup_res_add_none_kernel(tc, tab, base, w, offs, out):
    nc = tc.nc
    row_blocks, out_blocks = R // P, M // P
    tab_blocks = tab.rearrange("d (p k) s -> (d k) p s", p=P)
    base_rows = base.rearrange("(p k) n -> p (k n)", p=P)
    w_rows = w.rearrange("(p k) m -> p (k m)", p=P)
    out_rows = out.rearrange("(m p) n -> m p n", p=P)

    with (
        tc.tile_pool(name="held", bufs=1) as held,
        tc.tile_pool(name="x_halves", bufs=2 * row_blocks) as x_halves,
        tc.tile_pool(name="results", bufs=2 * out_blocks) as results,
        tc.psum_pool(name="psum", bufs=1) as psum,
    ):
        offsets = held.tile([P, N // 16], U16, name="offsets")
        nc.sync.dma_start(offsets[:], offs)
        windows = [held.tile([P, S], BF16, name=f"window{k}") for k in range(row_blocks)]
        bases = held.tile([P, row_blocks * N], BF16, name="bases")
        weights = held.tile([P, row_blocks * M], BF16, name="weights")
        nc.sync.dma_start(windows[0][:], tab_blocks[0, :, :])
        nc.sync.dma_start(bases[:], base_rows)
        nc.sync.dma_start(weights[:], w_rows)
        for k in range(1, row_blocks):
            nc.sync.dma_start(windows[k][:], tab_blocks[k, :, :])

        banks = [[psum.tile([P, HALF], F32, name=f"bank{h}_{m}") for m in range(out_blocks)] for h in range(2)]

        for k in range(row_blocks):
            for h in range(2):
                half_list = offsets[:, h * HALF // 16 : (h + 1) * HALF // 16]
                x = x_halves.tile([P, HALF], BF16, name="x")
                nc.vector.tensor_tensor(x[:], windows[k][:].indirect(half_list),
                                        bases[:, k * N + h * HALF : k * N + (h + 1) * HALF], mybir.AluOpType.add)
                for m in range(out_blocks):
                    nc.tensor.matmul(banks[h][m][:], weights[:, k * M + m * P : k * M + (m + 1) * P], x[:],
                                     start=(k == 0), stop=(k == row_blocks - 1))

        for h in range(2):
            for m in range(out_blocks):
                result = results.tile([P, HALF], F32, name="result")
                if h == 0:
                    nc.scalar.copy(result[:], banks[h][m][:])
                else:
                    nc.vector.tensor_copy(result[:], banks[h][m][:])
                nc.sync.dma_start(out_rows[m, :, h * HALF : (h + 1) * HALF], result[:])
